import numpy as np, ml_dtypes
CORES = [8,9,10,11,12,13]
N = 6
BF = ml_dtypes.bfloat16
W, NN, NL, P, C, ND, M, RO = 4096, 2048, 2048, 512, 64, 2, 8, 4
def look(E, wts, lim, q, D):
    u = (q @ wts) & 4095
    h = (u[:, 0] * u[:, 1]) >> 5
    slot = (h[:, None, None] + 613 * D[:, :, None] + np.arange(M)[None, None, :] * (2 * u[:, 0] + 1)[:, None, None]) & (W - 1)
    slot = slot.reshape(len(q), ND * M)
    dist = np.add.reduce(np.abs(E[slot] - q[:, None, :]), axis=2)
    ok = dist <= lim
    return np.where(np.any(ok, axis=1), slot[np.arange(len(q)), np.argmax(ok, axis=1)], -1), np.min(dist, axis=1)
def wish(NM, K, G):
    rho = np.add.reduce(G, axis=1) & 15
    return (NM[K[np.arange(len(K)), rho]] + G) & 255
def near(x, a, g):
    q = wish(x["NM"][a, g], x["L"][a, g][x["S"][a, g]], x["G"][a, g])
    return look(x["E"][a, g], x["WT"][a, g], 0, q, x["D"][a, g])[1]
def parts(rng):
    def w(hi, *shape): return rng.integers(0, hi, (N, 8) + shape, dtype=np.int32)
    return {"E": w(256, W, 16), "NM": w(256, NN, 16), "L": w(NN, NL, 16), "SG": w(NL, W), "DR": w(256, NL), "WT": w(256, 16, 2), "TH": 850 + w(350), "S": w(NL, P), "D": w(256, P, ND), "G": w(256, P, 16)}
def flat(v):
    return np.ascontiguousarray(v.transpose(0, 1, 3, 2)).reshape(N, 128, v.shape[2])
def tall(v):
    return np.ascontiguousarray(v.astype(np.float32).astype(np.int32).reshape(N, 8, 16, -1).transpose(0, 1, 3, 2))
def pack(x):
    def b(v): return flat(v).astype(np.float32).astype(BF)
    def i(v): return np.ascontiguousarray(v).astype(np.int32)
    return {"ent": b(x["E"]), "nm": b(x["NM"]), "lk": i(flat(x["L"])), "sg": i(x["SG"]), "dr": i(x["DR"]), "wt": i(x["WT"].reshape(N, 128, 2)), "th": i(np.repeat(x["TH"], 16, axis=1).reshape(N, 128, 1)),
            "s0": i(x["S"]), "d0": i(x["D"].transpose(0, 1, 3, 2).reshape(N, 8, ND * P)), "g0": b(x["G"])}
def setup_inputs(rng):
    return pack(parts(rng))
def setup_inputs_room(rng):
    x = parts(rng)
    for a in range(N):
        for g in range(8):
            v = near(x, a, g); lim = np.sort(v)[P // 2 - 1]; A = np.flatnonzero(v <= lim); B = np.flatnonzero(v > lim)
            x["TH"][a, g] = lim
            if len(B) == 0: continue
            n = int(rng.choice(np.array([0, 1, C - 1, C, C + 1, P])))
            if a == 0: n = (C, C + 1, P, C - 1, 1, 0, C, C + 1)[g]
            pick = rng.permutation(np.concatenate([rng.choice(A, P - n), rng.choice(B, n)]))
            for k in ("S", "D", "G"): x[k][a, g] = x[k][a, g][pick]
    return pack(x)
def setup_inputs_ties(rng):
    x = parts(rng)
    for k in ("E", "NM", "G"): x[k] = (x[k] >> 6) << 6
    x["TH"] = (64 * rng.integers(14, 18, (N, 8)) - (np.arange(8) & 1)[None, :]).astype(np.int32)
    r = N - 1
    x["TH"][r] = 4080; x["TH"][r, 5] = 2048; x["TH"][0, 5] = 4080
    for a in (r, 0): x["E"][a, 5] = x["E"][a, 5] & 64
    x["E"][r, 5, :, 0] = 0; x["NM"][r, 5] = 64; x["G"][r, 5] = x["G"][r, 5] & 64; x["G"][r, 5, ::2] = 128
    return pack(x)
def setup_inputs_alike(rng):
    x = parts(rng)
    for k in ("S", "D", "G"): x[k][:, 0] = x[k][:, 0, :1].copy()
    x["E"][:, 1] = x["E"][:, 1, :1].copy()
    x["SG"][:, 2] = rng.choice(np.array([0, NL - 1, 3]), (N, W))
    x["L"][:, 3] = rng.integers(0, NN, (N, 1, 1))
    x["D"][:, 4] = rng.integers(0, 256, (N, 1, 1))
    x["DR"][:, 5] = rng.integers(0, 256, (N, 1))
    x["WT"][:, 6] = 0
    x["E"][:, 7] = np.tile(x["E"][:, 7, :64].copy(), (1, W // 64, 1))
    return pack(x)
def setup_inputs_ends(rng):
    x = parts(rng); who = np.arange(N); even = who % 2 == 0; odd = ~even
    x["TH"][:, 0] = np.where(even, 4080, 0)
    x["NM"][odd, 0] = 0; x["G"][odd, 0, ::2] = 0; x["D"][odd, 0, ::4] = 0; x["L"][even, 0, ::2] = 0
    x["NM"][:, 1] = 0; x["TH"][:, 1] = 0; four = rng.integers(0, 256, (N, 4, 16))
    for a in range(N):
        x["E"][a, 1] = four[a][rng.integers(0, 4, W)]
        close = four[a].copy(); at = rng.integers(0, 16, 4); close[np.arange(4), at] = close[np.arange(4), at] ^ 1
        pool = np.concatenate([four[a], four[(a + 1) % N], close])
        x["G"][a, 1] = pool[rng.permutation(np.arange(P) % 12)]
    x["TH"][:, 2] = np.where(who == 0, 4080, np.where(who == 1, 4079, rng.integers(2000, 4079, N)))
    x["NM"][:, 2] = 0; x["E"][:, 2] = np.where(rng.random((N, W, 1)) < 0.5, 0, x["E"][:, 2]); x["G"][:, 2, ::2] = 255
    x["NM"][:, 3] = 0; x["WT"][:, 3] = 0; x["WT"][:, 3, 0] = 16; x["WT"][:, 3, 1] = 1; x["G"][:, 3, ::2, 0] = 255; x["G"][:, 3, ::2, 1] = 15
    x["L"][:, 4] = rng.choice(np.array([0, NN - 1]), (N, NL, 16)); x["SG"][:, 4] = rng.choice(np.array([0, NL - 1]), (N, W)); x["S"][:, 4] = rng.choice(np.array([0, NL - 1]), (N, P))
    x["DR"][:, 4] = rng.choice(np.array([0, 255]), (N, NL)); x["D"][:, 4] = rng.choice(np.array([0, 255]), (N, P, ND))
    for k in ("E", "NM", "G"): x[k][:, 5] = 255 * (x[k][:, 5] >> 7)
    x["TH"][:, 5] = 1529
    x["WT"][:, 6] = 255; x["NM"][:, 6] = 0; x["TH"][even, 6] = 4080
    x["G"][:, 6, ::2] = rng.integers(225, 256, (N, P // 2, 16)); x["G"][:, 6, 0] = 255
    x["TH"][:, 7] = 0
    return pack(x)
def setup_inputs_spread(rng):
    x = parts(rng)
    def col(n): return (np.exp2(rng.integers(0, 9, (N, 8, n, 1))) * rng.random((N, 8, n, 16))).astype(np.int32) * (rng.random((N, 8, n, 1)) > 0.0625)
    def low(hi, pw, *shape): return np.minimum((hi * rng.random((N, 8) + shape) ** pw).astype(np.int32), hi - 1)
    x["E"] = col(W); x["NM"] = col(NN); x["G"] = col(P)
    x["L"] = low(NN, 3, NL, 16); x["SG"] = low(NL, 2, W); x["DR"] = low(256, 2, NL); x["S"] = low(NL, 2, P); x["D"] = low(256, 3, P, ND)
    x["WT"] = np.minimum(np.exp2(8 * rng.random((N, 8, 16, 2))).astype(np.int32), 255)
    for a in range(N):
        for g in range(8):
            x["TH"][a, g] = np.sort(near(x, a, g))[int(rng.integers(P // 4, 3 * P // 4))]
    return pack(x)
def check_inputs(d):
    bad = []
    for k, hi in (("ent", 255), ("nm", 255), ("lk", NN - 1), ("sg", NL - 1), ("dr", 255), ("wt", 255), ("th", 4080), ("s0", NL - 1), ("d0", 255), ("g0", 255)):
        v = np.asarray(d[k]).astype(np.float64)
        if not (np.min(v) >= 0 and np.max(v) <= hi): bad.append("range of " + k)
        if np.any(v != np.floor(v)): bad.append("whole numbers in " + k)
    t = np.asarray(d["th"]).reshape(N, 8, 16)
    if np.any(t != t[:, :, :1]): bad.append("equal rows of a group in th")
    return bad
def reference(ent, nm, lk, sg, dr, wt, th, s0, d0, g0):
    E = tall(ent); NM = tall(nm); L = np.ascontiguousarray(lk.reshape(N, 8, 16, NL).transpose(0, 1, 3, 2)); WT = wt.astype(np.int32).reshape(N, 8, 16, 2)
    lim = th.reshape(N, 8, 16)[:, :, 0]
    G = tall(g0); D = np.array(d0.reshape(N, 8, ND, P).transpose(0, 1, 3, 2)).astype(np.int32)
    K = np.stack([np.stack([L[a, g][s0[a, g]] for g in range(8)]) for a in range(N)]).astype(np.int32)
    for step in range(RO):
        for a in range(N):
            b = (a + 1) % N
            for g in range(8):
                q = wish(NM[a, g], K[a, g], G[a, g])
                hit = look(E[a, g], WT[a, g], lim[a, g], q, D[a, g])[0]
                own = np.flatnonzero(hit >= 0); miss = np.flatnonzero(hit < 0)[:C]
                far = look(E[b, g], WT[b, g], lim[b, g], q[miss], D[a, g][miss])[0]
                G[a, g] = q
                for who, ix, slot in ((a, own, hit[own]), (b, miss[far >= 0], far[far >= 0])):
                    s = sg[who, g][slot]
                    G[a, g][ix] = E[who, g][slot]
                    K[a, g][ix] = L[who, g][s]
                    D[a, g][ix] = np.concatenate([dr[who, g][s][:, None], D[a, g][ix][:, :ND - 1]], axis=1)
    return {"yk": flat(K).astype(np.float32), "yd": np.ascontiguousarray(D.transpose(0, 1, 3, 2)).reshape(N, 8, ND * P).astype(np.float32), "yg": flat(G).astype(np.float32)}

import math
from concourse.mybir import AluOpType as A, AxisListType, ActivationFunctionType as F

STEPS = 4
NC = 12
LAG = 3.0
NENG = 16
SUMW = float(sum(2 ** (3 * j // 2) for j in range(16)))
PSUM = ("pa", "pb", "pc", "pd", "pe", "pf", "pg", "ph")
SB = {
    "bfloat16": "ENT 4672 NM 2048 SGT 4608 sgf 512 G0 512 DG 4096 I16 16 SA 144 SW1 144 SW2 144 SP 144 SM 144 BO 128 ID 128 TRI 128 LC 128 "
                "LZ 128 WB1 128 WB2 128 LO 128 HI 128 QC 128 tm 512 Gm 512 mask 512 sgh 512 Z 576 E 8192 E2 8192 ok 576 Qb 512 ob 192 "
                "orep 1024 od 1024 oa 1024 wb 64 cb 320 ask 512 askl 512 sbb 256 qrep 1024 sd 1024 sa 1024 rb 64 Dx 1024",
    "float16": "sdh 1536 SAh 144 S8h 144 km 512 sh 320",
    "int32": "LK 2240 sg2 512 sgi 256 dri 128 sdi 1536 wti 8 pci 8 qp 512 DS 64 vi 256 oi 576 X 512 X2 512 wi 512 DW 208 si 576 ri 128",
    "float32": "DRT 2240 drf 128 wtf 8 io144 144 io8 144 iog 128 iomp 128 iok 128 iopos 128 pcf 16 nrow 64 ncz 64 NCt 64 n4 16 pW 32 "
               "io512 512 q16 64 vf 192 of 256 wf 640 CW 72 ci 64 junk 128 sf 256 rf 256 Gf 576 Kf 576 Df 576",
    "uint16": "nu 64 ou 64 OFF 512 wu 192 cu 32 rep 800 repl 800 su 80",
}
SCRATCH = {}
for _d, _s in SB.items():
    for _n, _w in zip(_s.split()[0::2], _s.split()[1::2]):
        SCRATCH[_n] = ("sbuf", [128, int(_w)], _d)
for _p in PSUM:
    SCRATCH[_p] = ("psum", [128, 512], "float32")
SEMAPHORES = ["sv", "ss", "st", "sg_", "sent"] + ["d%d" % k for k in range(19)] + ["a%d" % k for k in range(4)] + ["r%d" % k for k in range(4)]

CYC, PEC, HOP, GAT, SCA, RLAT = 1.04, 0.55, 110.0, 1.56, 3.8, 2500.0
ROUNDS, TEMP = 45000, 500.0


def R(name, a=0, b=None, step=1, parts=None):
    return ("r", name, a, SCRATCH[name][1][1] if b is None else b, step, parts)


def C(name, a):
    return ("r", name, a, a + 1, 1, None)


def IND(win, off):
    return ("ind", win, off)


def width(r):
    if r[0] == "ind":
        return 16 * (r[2][3] - r[2][2])
    return len(range(r[2], r[3], r[4]))


def size(r):
    return 4 if SCRATCH[r[1]][2] in ("float32", "int32") else 2


def build():
    ops = []
    acc = {}

    def add(eng, calls, outs, ins, cost, lat=0.0, kind="c", extra=None):
        me = len(ops)
        deps = set()
        touch = []
        for rs, mode in ((ins, "r"), (outs, "w")):
            for r in rs:
                if isinstance(r, tuple) and r[0] == "ind":
                    touch += [(r[1], mode), (r[2], "r")]
                elif isinstance(r, tuple) and r[0] == "r":
                    touch.append((r, "s" if mode == "w" and r[4] == 16 else mode))
        for r, mode in touch:
            ps = r[1] in PSUM
            for (o, l2, h2, m2, e2) in acc.get(r[1], []):
                if o == me or ((l2 >= r[3] or r[2] >= h2) and not (ps and (e2 != eng or eng == "t"))):
                    continue
                if (mode == "r" and m2 == "r" and not (ps and e2 != eng)) or (mode == "s" and m2 == "s"):
                    continue
                deps.add(o)
        for r, mode in touch:
            lst = acc.setdefault(r[1], [])
            if mode == "w":
                lst[:] = [x for x in lst if x[0] == me or not (x[1] >= r[2] and x[2] <= r[3])]
            lst.append((me, r[2], r[3], mode, eng))
        ops.append({"eng": eng, "calls": calls, "deps": deps, "cost": cost, "lat": lat, "kind": kind, "extra": extra})

    def vcost(out, ins, two=False):
        n = width(out)
        if out[0] == "ind":
            return 50 + SCA * n * CYC
        full = [r for r in ins if isinstance(r, tuple) and width(r) == n]
        if any(r[0] == "ind" for r in full):
            return 50 + GAT * n * CYC
        f = 1.0
        if two:
            f = 1.0 if any(r[1] in PSUM for r in full) else 2.0
        elif size(out) == 2 and all(size(r) == 2 for r in full):
            f = 0.5
        return max(64, n * f) * CYC

    def cp(out, in_):
        add("v", [("tensor_copy", [out, in_], {})], [out], [in_], vcost(out, [in_]))

    def tt(out, a, b, op):
        add("v", [("tensor_tensor", [out, a, b, op], {})], [out], [a, b], vcost(out, [a, b], True))

    def ts(out, a, s1, op0, s2=None, op1=None):
        add("v", [("tensor_scalar", [out, a, s1, s2, op0] + ([op1] if op1 is not None else []), {})], [out], [a, s1, s2], vcost(out, [a]))

    def ms(out, val):
        add("v", [("memset", [out, val], {})], [out], [], vcost(out, []))

    def scan(out, a, b, init, op0, op1):
        add("v", [("tensor_tensor_scan", [out, a, b, init, op0, op1], {})], [out], [a, b], 70.0)

    def act(out, in_, func, bias=None, scale=None, accum_out=None, more=0.0):
        kw = {k: v for k, v in (("bias", bias), ("scale", scale), ("accum_out", accum_out)) if v is not None}
        n = width(out)
        cost = 65 + GAT * n * CYC if in_[0] == "ind" else max(64, n) * CYC
        add("s", [("activation", [out, in_, func], kw)], [out, accum_out], [in_, bias, scale], cost + more)

    def iota(out, pattern, base=0, cm=0):
        kw = {} if SCRATCH[out[1]][2] == "int32" else {"allow_small_or_imprecise_dtypes": True}
        add("g", [("iota", [out, pattern, base, cm], kw)], [out], [], 130 + 2 * width(out) * CYC)

    def mm(*groups, first=True, close=True):
        calls, outs, ins, cost = [], [], [], 0.0
        for grp in groups:
            for k, (o, l, r) in enumerate(grp):
                calls.append(("matmul", [o, l, r, k == 0 and first, k == len(grp) - 1 and close], {}))
                outs.append(o)
                ins += [l, r]
                cost += max(64, width(r)) * PEC
        add("t", calls, outs, ins, cost)

    def wrapg(out, strip, src, a, n, parts=None):
        return [(out, R(strip, 16 - r, 144 - r, 1, parts), R(src, a + r, a + n, 16, parts)) for r in range(16)]

    ndma = [0]

    def dma(eng, out, in_, lat):
        add(eng, [("dma_start", [out, in_], {})], [out], [in_], 60.0, lat, "d", "d%d" % ndma[0])
        ndma[0] += 1

    def remote(dst, src, sem, step):
        add("g", [("remote", [dst, src, sem, step], {})], [dst], [src], 300.0, RLAT, "x")

    def H(name, sl=None):
        return ("hbm", name, sl)

    P8, ROW0, ROW1 = (0, 8, 1), (0, 128, 16), (1, 128, 16)
    dma("y", R("sdi", 0, 512, 1, P8), H("s0"), 2000)
    dma("y", R("G0"), H("g0"), 2300)
    dma("y", R("LK", 0, 2048), H("lk"), 5500)
    dma("y", R("NM"), H("nm"), 7000)
    dma("y", R("ENT", 0, 4096), H("ent"), 10000)
    dma("s", R("wti", 0, 2), H("wt"), 2000)
    dma("s", R("sdi", 512, 1536, 1, P8), H("d0"), 2200)
    dma("s", C("wti", 4), H("th"), 2200)
    dma("y", R("sgi"), H("sg"), 10500)
    dma("y", R("dri"), H("dr"), 10800)

    eq, mul, plus, sub, band, shr = A.is_equal, A.mult, A.add, A.subtract, A.bitwise_and, A.logical_shift_right
    iota(R("io8", 0, 144, 1, P8), [[1, 144]], -16, -16)
    ts(R("S8h", 0, 144, 1, P8), R("io8", 0, 144, 1, P8), 0.0, eq)
    iota(C("pci", 0), [[0, 1]], 0, 1)
    iota(R("io144"), [[1, 144]], -16, 0)
    iota(R("nrow"), [[1, 64]])
    for k, m in ((1, 15), (2, 112), (3, 7)):
        ts(C("pci", k), C("pci", 0), m, band)
    cp(R("pcf", 0, 4), R("pci", 0, 4))
    pm, g16, mcol, mcol2, sel1, pw = [C("pcf", k) for k in range(1, 7)]
    w1, w2, th, thh = C("wtf", 0), C("wtf", 1), C("wtf", 4), C("wtf", 5)
    BO, ID, nrow, iomp = R("BO"), R("ID"), R("nrow"), R("iomp")
    ts(mcol2, mcol, 2.0, mul)
    ts(sel1, pm, 1.0, eq)
    ts(R("SA"), R("io144"), g16, eq)
    ts(R("SAh"), R("io144"), g16, eq)
    ts(R("I16"), R("nrow", 0, 16), pm, eq)
    cp(R("wtf", 0, 2), R("wti", 0, 2))
    cp(th, C("wti", 4))
    ts(thh, th, 0.5, plus)
    ms(R("q16", 0, 16), 2.0)
    ms(R("q16", 2, 16, 2), 4.0)
    ms(R("q16", 48, 64), 0.0)
    scan(R("q16", 16, 32), R("q16", 0, 16), R("q16", 48, 64), 0.5, mul, plus)
    ts(R("q16", 32, 48), R("nrow", 0, 16), pm, plus, 15.0, eq)
    tt(R("q16", 32, 48), R("q16", 16, 32), R("q16", 32, 48), mul)
    add("v", [("tensor_reduce", [pw, R("q16", 32, 48), AxisListType.X, plus], {})], [pw], [R("q16", 32, 48)], 70.0)
    for strip, w in (("SW1", w1), ("SW2", w2), ("SM", -2.0), ("SP", pw)):
        ts(R(strip), R("io144"), g16, eq, w, mul)
    iota(iomp, [[1, 128]], 0, -1)
    iota(R("iog"), [[16, 8], [0, 16]])
    iota(R("iopos"), [[0, 8], [1, 2], [2, 8]])
    iota(R("iok"), [[0, 8], [1, 16]])
    ts(ID, iomp, 0.0, eq)
    ts(BO, R("iog"), g16, eq)
    tm = [R("tm", 128 * k, 128 * k + 128) for k in range(4)]
    ts(tm[0], R("iopos"), float(NC), A.is_lt)
    tt(R("QC"), tm[0], BO, mul)
    ts(tm[1], iomp, 0.0, A.is_gt, -1.0, mul)
    tt(tm[1], tm[1], BO, mul)
    tt(R("TRI"), tm[1], ID, plus)
    ts(tm[2], iomp, 0.0, A.is_lt, -1.0, mul)
    tt(R("LC"), tm[2], BO, mul)
    ts(tm[3], ID, -1024.0, mul)
    tt(R("LZ"), tm[3], R("LC"), plus)
    ts(R("WB1"), BO, w1, mul)
    ts(R("WB2"), BO, w2, mul)
    ts(tm[0], R("iok"), 8.0, A.is_lt)
    tt(R("LO"), tm[0], BO, mul)
    tt(R("HI"), BO, R("LO"), sub)
    ts(R("ncz"), nrow, -1023.0, plus)
    ts(R("NCt"), nrow, 1.0, plus, 256.0, mul)
    ts(R("NCt"), R("NCt"), sel1, mul)
    cp(R("nu"), nrow)
    ts(R("n4", 0, 4), R("nrow", 0, 64, 16), pm, plus, 512.0, plus)
    ts(R("n4", 4, 8), R("nrow", 0, 64, 16), pm, plus, 0.5, plus)
    ts(R("pW"), R("nrow", 0, 32), 16.0, mul, pm, plus)
    ts(R("pW"), R("pW"), 4096.0, plus)
    ms(R("ENT", 4608, 4672), 0.0)
    ms(R("CW", 64, 72), 4096.0)
    ms(R("DW", 96, 104), 0)
    ms(R("DW", 200, 208), 0)
    for x in ("Z", "ok", "Gf", "Kf", "Df"):
        ms(R(x, 512, 576), 0.0)
    for k in range(4):
        iota(R("SGT", 1152 * k, 1152 * k + 1152), [[0, 1152]])
    for k in range(2):
        iota(R("DRT", 1120 * k, 1120 * k + 1120), [[0, 1120]])
    iota(R("io512"), [[0, 32], [1, 16]])
    ts(R("DG", 0, 512), R("io512"), pm, eq)
    for k in range(1, 8):
        act(R("DG", 512 * k, 512 * k + 512), R("DG", 0, 512), F.Copy)
    ts(R("sg2", 0, 256), R("sgi"), 63, band)
    ts(R("sg2", 256, 512), R("sgi"), 1984, band)
    cp(R("sgf"), R("sg2"))
    cp(R("drf"), R("dri"))
    dma("y", R("SGT", 0, 4096, 1, ROW0), R("sgf", 0, 256), 2500)
    dma("y", R("SGT", 0, 4096, 1, ROW1), R("sgf", 256, 512), 2500)
    dma("y", R("DRT", 0, 2048, 1, ROW0), R("drf"), 2500)

    Q, QW, Qb, ENT = R("ENT", 4096, 4608), R("ENT", 4096, 4672), R("Qb"), R("ENT", 0, 4096)

    def wi(k, n=1):
        return R("wi", 32 * k, 32 * (k + n))

    def wf(k, n=1):
        return R("wf", 32 * k, 32 * (k + n))

    def wu(k, lo=0, hi=32):
        return R("wu", 32 * k + lo, 32 * k + hi)

    S = wf(0)
    SU, CU, IU, RU = 0, 1, 2, 3
    HV = ((0, 256, 0, 16), (256, 512, 16, 32))

    def names(lkw, G):
        mm(wrapg(R("pe", 0, 32), "SA", G, 0, 512))
        if G == "G0":
            cp(wi(0), R("pe", 0, 32))
            ts(wi(1), wi(0), 15, band)
            cp(wu(RU), wi(1))
        else:
            cp(wu(RU), R("pe", 0, 32))
        for a, b, c, d in HV:
            act(R("mask", a, b), IND(R("I16" if G == "G0" else "DG"), wu(RU, c, d)), F.Copy)
            tt(R("km", a, b), IND(R("LK", 0, lkw), wu(SU, c, d)), R("mask", a, b), mul)
        mm(wrapg(R("pc", 0, 32), "SAh", "km", 0, 512))
        cp(wu(CU), R("pc", 0, 32))
        for a, b, c, d in HV:
            tt(R("qp", a, b), IND(R("NM"), wu(CU, c, d)), R(G, a, b), plus)
            ts(R("qp", a, b), R("qp", a, b), 255, band)
            cp(R("Qb", a, b), R("qp", a, b))
        mm([(R("pb"), ID, Qb)])
        act(Q, Qb, F.Copy)

    def s64(x, k, n=1):
        return R(x, 64 * k, 64 * (k + n))

    def look(aq, aD, ps, ni, nf, nu, qr, sd, sa):
        mm([(R(ps, 0, 64), R("WB1"), aq)], [(R(ps, 64, 128), R("WB2"), aq)])
        for h in range(16):
            act(R(qr, h, 1024, 16), aq, F.Copy)
        act(s64(nf, 0), aD, F.Identity, scale=613.0)
        cp(s64(ni, 0, 2), R(ps, 0, 128))
        ts(s64(ni, 2, 2), s64(ni, 0, 2), 4095, band)
        act(s64(nf, 1), R(ps, 0, 64), F.Identity, bias=mcol, scale=mcol2)
        tt(s64(ni, 4), s64(ni, 2), s64(ni, 3), mul)
        tt(s64(nf, 2), s64(nf, 1), s64(nf, 0), plus)
        ts(s64(ni, 5), s64(ni, 4), 5, shr)
        tt(s64(ni, 6), s64(ni, 5), s64(nf, 2), plus)
        ts(s64(ni, 7), s64(ni, 6), 4095, band)
        cp(R(nu, 0, 64), s64(ni, 7))
        for h in range(4):
            a, b = 256 * h, 256 * h + 256
            tt(R(sd, a, b), IND(ENT, R(nu, 16 * h, 16 * h + 16)), R(qr, a, b), sub)
            act(R(sa, a, b), R(sd, a, b), F.Abs)
        mm(wrapg(R(ps, 0, 64), "SA", sa, 0, 1024))

    def shift(fa, d0, out):
        tt(wf(14, 2), R("DW", d0, d0 + 64), R("DW", d0 + 32, d0 + 96), sub)
        for d in range(2):
            tt(wf(14 + d), wf(14 + d), fa, mul)
        tt(out, wf(14, 2), R("DW", d0 + 32, d0 + 96), plus)

    cn, pidx, off = R("cu", 0, 4), R("cu", 8, 12), R("cu", 16, 20)
    miss, incl, found, base0 = R("wb", 0, 32), R("wb", 32, 64), wf(5), R("vf", 64, 96)

    def merge(t):
        rk, lkw, d0 = 200 * t, 2048 + 64 * t, 104 * (t % 2)
        d1 = 104 - d0
        cp(R("rf", 0, 128), R("repl", rk, rk + 128))
        tt(s64("ri", 0), IND(R("NM"), R("repl", rk + 196, rk + 200)), s64("rf", 0), plus)
        ts(s64("ri", 1), s64("ri", 0), 255, band)
        cp(s64("ob", 0), s64("ri", 1))
        cp(s64("ob", 1), s64("rf", 1))
        mm([(R("pg", 0, 64), R("LO"), s64("ob", 1)), (R("pg", 0, 64), R("HI"), s64("cb", 2))])
        look(s64("ob", 0), R("pg", 0, 64), "pf", "oi", "of", "ou", "orep", "od", "oa")
        act(s64("ob", 2), R("pf", 0, 64), F.Sign, bias=thh, scale=-1.0)
        tt(R("rb"), s64("rf", 1), R("NCt"), plus)
        cp(IND(R("Z"), off), R("rb"))
        cp(IND(QW, off), s64("ob", 0))
        cp(R("LK", lkw, lkw + 64), R("repl", rk + 128, rk + 192))
        mm(wrapg(R("pe", 0, 32), "SA", "Z", 0, 512))
        cp(wi(12), R("pe", 0, 32))
        ts(wf(16), R("pe", 0, 32), 256.0, A.is_ge)
        ts(R("DW", d0, d0 + 32), wi(12), 255, band)
        tt(wf(17), wf(16), found, plus)
        shift(wf(17), d0, R("DW", d1 + 32, d1 + 96))
        ts(wi(13), wi(12), 8, shr)
        ts(wf(18), wi(13), float(lkw - 1), plus)
        tt(wf(18), wf(18), S, sub)
        tt(wf(18), wf(18), wf(16), mul)
        tt(S, S, wf(18), plus)
        mm(wrapg(R("pe", 0, 32), "SW1", "ENT", 4096, 512))
        mm(wrapg(R("pe", 32, 64), "SW2", "ENT", 4096, 512))
        ts(s64("vf", 0), R("DW", d1 + 32, d1 + 96), 613.0, mul)
        cp(s64("vi", 0), R("pe", 0, 64))
        ts(s64("vi", 1), s64("vi", 0), 4095, band)
        tt(R("vi", 128, 160), R("vi", 64, 96), R("vi", 96, 128), mul)
        ts(R("vi", 160, 192), R("vi", 128, 160), 5, shr, 4095, band)
        tt(base0, R("vi", 160, 192), R("vf", 0, 32), plus)
        ts(wf(19), R("vi", 64, 96), -16.0, mul, -8.0, plus)
        tt(wf(4), R("vf", 32, 64), R("vf", 0, 32), sub)
        tt(wf(4), wf(4), wf(19), plus)
        ts(wf(3), R("vi", 64, 96), 2.0, mul, 1.0, plus)
        cp(IND(R("ok"), off), s64("ob", 2))

    for k in range(3):
        cp(R("sdh", 512 * k, 512 * k + 512, 1, P8), R("sdi", 512 * k, 512 * k + 512, 1, P8))
    mm(wrapg(R("pc", 0, 32), "S8h", "sdh", 0, 512, P8))
    cp(wu(SU), R("pc", 0, 32))
    cp(S, R("pc", 0, 32))
    mm(wrapg(R("pf", 0, 64), "S8h", "sdh", 512, 1024, P8))
    cp(R("DW", 32, 96), R("pf", 0, 64))
    names(2048, "G0")

    for t in range(STEPS):
        last = t == STEPS - 1
        d0, lkw, ak, rk = 104 * (t % 2), 2048 + 64 * t, 128 * t, 200 * t
        d1 = 104 - d0
        mm(wrapg(R("pd", 0, 32), "SW1", "Qb", 0, 512))
        mm(wrapg(R("pd", 32, 64), "SW2", "Qb", 0, 512))
        mm([(R("pa"), R("QC"), Qb)], close=False)
        ts(wf(1, 2), R("DS") if t else R("DW", 32, 96), 613.0, mul)
        cp(wi(2, 2), R("pd", 0, 64))
        for c in range(2, 16):
            act(R("pd", 32 * c, 32 * c + 32), R("pd", 0, 32), F.Identity, bias=float(c // 2), scale=float(2 * (c // 2)))
        ts(wi(4, 2), wi(2, 2), 4095, band)
        tt(wi(6), wi(4), wi(5), mul)
        ts(wi(7), wi(6), 5, shr, 4095, band)
        for d in range(2):
            tt(R("X", 32 * d, 32 * d + 32), wi(7), wf(1 + d), plus)
        for m in range(1, 8):
            tt(s64("X", m), s64("X", 0), s64("pd", m), plus)
        for a, b in ((0, 64), (64, 192), (192, 352), (352, 512)):
            ts(R("X2", a, b), R("X", a, b), 4095, band)
            cp(R("OFF", a, b), R("X2", a, b))
        if t == 0:
            ts(wf(3), wi(4), 2.0, mul, 1.0, plus)
            ts(wf(19), wi(4), -16.0, mul, -8.0, plus)
            tt(wf(4), R("X", 32, 64), R("X", 0, 32), sub)
            tt(wf(4), wf(4), wf(19), plus)
            cp(base0, R("X", 0, 32))
        seq = sorted(range(16), key=lambda x: (x + 0.5) / NC if x < NC else (x - NC + LAG) / (16 - NC + LAG))
        for pos in seq:
            k = 8 * (pos % 2) + pos // 2
            e, e2 = R("E", 512 * pos, 512 * pos + 512), R("E2", 512 * pos, 512 * pos + 512)
            src = IND(ENT, R("OFF", 32 * pos, 32 * pos + 32))
            grp = [(R("pa"), R("SA", 16 - k, 144 - k), e if pos < NC else e2)]
            if pos < NC:
                act(e, src, F.Copy)
                tt(e2, e, R("pb"), A.min)
                grp.append((R("pa"), R("SM", 16 - k, 144 - k), e2))
            else:
                tt(e, src, Qb, sub)
                act(e2, e, F.Abs)
            mm(grp, first=False, close=pos == seq[-1])
        act(R("ok", 0, 512), R("pa"), F.Sign, bias=thh, scale=-1.0)
        if t:
            merge(t - 1)
        B = R("pc", 0, 32)
        mm(wrapg(B, "SP", "ok", 0, 512))
        ts(miss, B, 1.0 - SUMW, A.is_lt)
        ts(found, B, 1.0 - SUMW, A.is_ge)
        ts(wf(7), B, 8191.0 - SUMW, A.is_lt)
        act(wf(6), B, F.Ln, bias=SUMW / 2 + 0.25, scale=0.5, more=1300.0 if t == 0 else 0.0)
        scan(incl, miss, miss, 0.0, plus, A.max)
        mm([(R("pf", 0, 32), BO, incl)])
        mm([(R("pg", 32, 64), BO, incl), (R("pg", 32, 64), R("LC"), miss)], [(R("pg", 0, 32), BO, incl), (R("pg", 0, 32), R("LZ"), miss)])
        for a in range(4):
            act(R("junk", 32 * a, 32 * a + 32), R("pf", 0, 32), F.Sign, bias=C("n4", 4 + a), scale=-1.0, accum_out=C("ci", a), more=20.0)
        cp(R("CW", 0, 64), R("pg", 0, 64))
        ts(cn, R("ci", 0, 4), 32.0, plus, 0.5, mul)
        ts(R("cb", 256, 260), R("ci", 0, 4), 32.0, plus, 8.0, mul)
        tt(s64("cb", 0), IND(R("CW", 32, 72), cn), nrow, A.is_le)
        tt(s64("cb", 1), IND(R("CW", 0, 40), cn), R("ncz"), eq)
        p4 = R("pf", 0, 4)
        mm([(p4, ID, R("cb", 256, 260))] + wrapg(p4, "SA", "cb", 0, 64))
        cp(pidx, p4)
        cp(R("ask", ak, ak + 64), IND(QW, pidx))
        for d in range(2):
            tt(s64("cb", 2 + d), IND(R("DW", d0 + 32 + 32 * d, d0 + 72 + 32 * d), cn), s64("cb", 1), mul)
        mm([(R("pg", 0, 64), R("LO"), s64("cb", 2)), (R("pg", 0, 64), R("HI"), s64("cb", 3))])
        act(R("ask", ak + 64, ak + 128), R("pg", 0, 64), F.Copy)
        remote(R("askl", ak, ak + 128), R("ask", ak, ak + 128), "a%d" % t, 1)
        tt(R("ci", 8, 12), p4, R("n4", 0, 4), sub)
        ts(R("ci", 16, 20), p4, 512.0, A.is_lt)
        tt(R("ci", 24, 28), R("ci", 8, 12), R("ci", 16, 20), mul)
        tt(wf(9), wf(7), wf(4), mul)
        tt(wf(9), wf(9), base0, plus)
        ts(wi(8), wf(6), -1.0 / (1.5 * math.log(2.0)), mul, 15.0, plus)
        tt(wf(8), wi(8), wf(3), mul)
        tt(wi(10), wf(8), wf(9), plus)
        ts(wi(11), wi(10), 4095, band)
        tt(wf(10), miss, R("pW"), mul)
        tt(wf(12), wi(11), wf(10), A.max)
        cp(wu(IU), wf(12))
        tt(wf(13), S, miss, mul)
        for x, win in (("Gf" if last else "Gm", R("ENT", 0, 4608)), ("sgh", R("SGT"))):
            act(R(x, 0, 256), IND(win, wu(IU, 0, 16)), F.Copy)
            cp(R(x, 256, 512), IND(win, wu(IU, 16, 32)))
        mm(wrapg(B, "SA", "sgh", 0, 512))
        tt(S, wf(13), B, plus)
        cp(wu(SU), S)
        for a, b, c, d in HV:
            act(R("Z", a, b), IND(R("DRT"), wu(SU, c, d)), F.Copy)
            if last:
                cp(R("Kf", a, b), IND(R("LK", 0, lkw), wu(SU, c, d)))
        if not last:
            names(lkw, "Gm")
        mm(wrapg(R("pe", 0, 32), "SA", "Z", 0, 512))
        cp(R("DW", d0, d0 + 32), R("pe", 0, 32))
        shift(found, d0, R("DW", d1 + 32, d1 + 96) if last else R("DS"))
        if last:
            for d in range(2):
                for a, b, c, e in HV:
                    tt(R("Dx", 512 * d + a, 512 * d + b), IND(R("DW", d1 + 32 + 32 * d, d1 + 64 + 32 * d), R("nu", c, e)), R("DG", a, b), mul)
            mm([(R("pb"), R("SA", 16, 144), R("Dx", 0, 512)), (R("pb"), R("SA", 15, 143), R("Dx", 512, 1024))])
            act(R("Df", 0, 512), R("pb"), F.Copy)
        look(R("askl", ak, ak + 64), R("askl", ak + 64, ak + 128), "ph", "si", "sf", "su", "qrep", "sd", "sa")
        ts(s64("sh", 2), s64("si", 7), -2048.0, plus)
        ts(s64("sbb", 0), R("ph", 0, 64), th, A.is_le)
        mm([(R("ph", 0, 64), R("TRI"), s64("sbb", 0))])
        ts(s64("sh", 1), R("ph", 0, 64), 1.0, A.is_ge)
        tt(s64("sh", 0), s64("sh", 1), s64("sh", 2), mul)
        mm(wrapg(R("ph", 0, 8), "SAh", "sh", 0, 128))
        t4, s4, h4 = R("su", 64, 68), R("su", 72, 76), R("ph", 0, 4)
        ts(t4, h4, 2048.0, plus)
        cp(R("rep", rk + 192, rk + 196), R("ph", 4, 8))
        cp(s64("sbb", 3), IND(R("SGT", 0, 4096), t4))
        act(s64("sf", 3), IND(ENT, t4), F.Copy)
        cp(R("rep", rk, rk + 64), s64("sf", 3))
        mm(wrapg(h4, "SA", "sbb", 192, 64))
        cp(s4, h4)
        if not last:
            act(s64("sbb", 1), IND(ENT, t4), F.Copy)
            mm([(R("pg", 0, 64), BO, s64("sbb", 1))])
            cp(s64("si", 0), R("pg", 0, 64))
            ts(s64("si", 1), s64("si", 0), 15, band)
            ts(s64("sbb", 2), s64("si", 1), pm, eq)
            tt(s64("sh", 4), IND(R("LK", 0, 2048), s4), s64("sbb", 2), mul)
            mm(wrapg(h4, "SAh", "sh", 256, 64))
            cp(R("rep", rk + 196, rk + 200), h4)
        cp(R("rep", rk + 64, rk + 128), IND(R("DRT", 0, 2048), s4))
        cp(R("rep", rk + 128, rk + 192), IND(R("LK", 0, 2048), s4))
        rw = 196 if last else 200
        remote(R("repl", rk, rk + rw), R("rep", rk, rk + rw), "r%d" % t, -1)
        for a in range(4):
            ts(C("cu", 16 + a), C("repl", rk + 192 + a), C("ci", 24 + a), mul, C("n4", a), plus)
        if last:
            ts(s64("rf", 3), R("ask", ak + 64, ak + 128), sel1, mul)
            cp(R("rf", 0, 192), R("repl", rk, rk + 192))
            cp(IND(R("Kf"), off), s64("rf", 2))
            dma("y", H("yk"), R("Kf", 0, 512), 3000)
            cp(IND(R("Gf"), off), s64("rf", 0))
            dma("s", H("yg"), R("Gf", 0, 512), 3000)
            tt(s64("rf", 3), s64("rf", 3), s64("rf", 1), plus)
            cp(IND(R("Df"), off), s64("rf", 3))
            dma("y", H("yd", (0, 512)), R("Df", 0, 512, 1, ROW0), 2200)
            dma("s", H("yd", (512, 1024)), R("Df", 0, 512, 1, ROW1), 2200)
    return ops


def schedule(ops):
    n = len(ops)
    succ = [[] for _ in ops]
    for i, o in enumerate(ops):
        for d in o["deps"]:
            succ[d].append(i)
    key = [0.0] * n
    for i in range(n - 1, -1, -1):
        key[i] = ops[i]["cost"] + ops[i]["lat"] + HOP + max([key[j] for j in succ[i]] + [0.0])
    left = [len(o["deps"]) for o in ops]
    ready = [0.0] * n
    cand, free, order = {}, {}, []
    for i in range(n):
        if left[i] == 0:
            cand.setdefault(ops[i]["eng"], []).append(i)
    while len(order) < n:
        best = None
        for e, lst in cand.items():
            if not lst:
                continue
            if e == "y":
                pick = min(lst)
            else:
                now = max(free.get(e, 0.0), min(ready[i] for i in lst))
                pick = max([i for i in lst if ready[i] <= now], key=lambda i: key[i])
                for j in lst:
                    if now < ready[j] < now + ops[pick]["cost"] and key[j] > key[pick] + ops[pick]["cost"] + (ready[j] - now):
                        pick = j
            st = max(free.get(e, 0.0), ready[pick])
            if best is None or st < best[0]:
                best = (st, e, pick)
        st, e, i = best
        cand[e].remove(i)
        free[e] = st + ops[i]["cost"]
        order.append(i)
        for j in succ[i]:
            ready[j] = max(ready[j], free[e] + ops[i]["lat"] + (0.0 if e == "t" and ops[j]["eng"] == "t" else HOP))
            left[j] -= 1
            if left[j] == 0:
                cand.setdefault(ops[j]["eng"], []).append(j)
    return order


def improve(ops, order, rounds):
    n = len(ops)
    eng = [o["eng"] for o in ops]
    cost = [o["cost"] for o in ops]
    tail = [o["cost"] + o["lat"] for o in ops]
    deps = [[(d, 0.0 if eng[d] == "t" and o["eng"] == "t" else HOP) for d in sorted(o["deps"])] for o in ops]

    def run(seq):
        free, prev = {}, {}
        st, fin, why = [0.0] * n, [0.0] * n, [-1] * n
        for i in seq:
            e = eng[i]
            t, w = free.get(e, 0.0), -2 - prev.get(e, -1)
            for d, h in deps[i]:
                if fin[d] + h > t:
                    t, w = fin[d] + h, d
            st[i], why[i] = t, w
            free[e], prev[e], fin[i] = t + cost[i], i, t + tail[i]
        end = max(fin)
        i = fin.index(end)
        pairs = []
        while i >= 0:
            w = why[i]
            if w < -1:
                w = -2 - w
                if eng[i] != "y":
                    pairs.append((w, i))
            i = w
        return end, st, pairs

    cur, st, pairs = run(order)
    best, keep, x = cur, list(order), 987654321
    for r in range(rounds):
        if not pairs:
            break
        x = (x * 1103515245 + 12345) % 2147483648
        a, b = pairs[(x >> 8) % len(pairs)]
        pa, pb = order.index(a), order.index(b)
        x = (x * 1103515245 + 12345) % 2147483648
        mid = order[pa:pb + 1]
        if (x >> 12) & 1:
            take = {b}
            for i in reversed(mid):
                if i in take:
                    take.update(d for d, _ in deps[i])
            if a in take:
                continue
            seq = order[:pa] + [i for i in mid if i in take] + [i for i in mid if i not in take] + order[pb + 1:]
        else:
            take = {a}
            for i in mid:
                if any(d in take for d, _ in deps[i]):
                    take.add(i)
            if b in take:
                continue
            seq = order[:pa] + [i for i in mid if i not in take] + [i for i in mid if i in take] + order[pb + 1:]
        end, st2, pairs2 = run(seq)
        x = (x * 1103515245 + 12345) % 2147483648
        if end <= cur - TEMP * (1.0 - r / rounds) * math.log((x + 1) / 2147483649.0):
            rank = {i: k for k, i in enumerate(seq)}
            order = sorted(seq, key=lambda i: (st2[i], rank[i]))
            cur, pairs = end, pairs2
            if cur < best:
                best, keep = cur, list(order)
    st = run(keep)[1]
    return best, [(st[i], i) for i in keep]


PLAN = {}


def plan():
    if not PLAN:
        PLAN["ops"] = build()
        PLAN["end"], PLAN["order"] = improve(PLAN["ops"], schedule(PLAN["ops"]), ROUNDS)
    return PLAN


def rank_program(g, core, T, topo):
    rank = T.rank_of(core)
    if rank is None:
        return
    ops = plan()["ops"]
    queue = {"v": g.vector, "s": g.scalar, "t": g.tensor, "g": g, "y": g.sync}
    esem = {"v": "sv", "s": "ss", "t": "st", "g": "sg_"}
    v = g.vector
    call = {"matmul": g.tensor.matmul, "tensor_copy": v.tensor_copy, "tensor_tensor": v.tensor_tensor, "tensor_scalar": v.tensor_scalar,
            "tensor_tensor_scan": v.tensor_tensor_scan, "tensor_reduce": v.tensor_reduce, "memset": v.memset,
            "activation": g.scalar.activation, "iota": g.iota}

    def ap(r):
        if isinstance(r, tuple) and r[0] == "r":
            p = r[5] or (0, 128, 1)
            return T[r[1]][p[0]:p[1]:p[2], r[2]:r[3]:r[4]]
        if isinstance(r, tuple) and r[0] == "ind":
            return ap(r[1]).indirect(ap(r[2]))
        if isinstance(r, tuple) and r[0] == "hbm":
            return T[r[1]][:] if r[2] is None else T[r[1]][:, r[2][0]:r[2][1]]
        return r

    total, done, waited = {}, {}, {}
    for _, i in plan()["order"]:
        o = ops[i]
        e = o["eng"]
        need = {}
        for d in o["deps"]:
            if e != "t" or ops[d]["eng"] != "t":
                s, val = done[d]
                need[s] = max(need.get(s, 0), val)
        for s in sorted(need):
            if waited.get((e, s), 0) < need[s]:
                queue[e].wait_ge(T.sem[s], need[s])
                waited[(e, s)] = need[s]
        for name, args, kw in o["calls"]:
            if name == "remote":
                dst = T.cores[(rank + args[3]) % len(T.cores)]
                rid, pid = topo.addr(dst)[0:2]
                eng = topo.engines(core, dst)[0:NENG]
                g.remote_dma(ap(args[0]), ap(args[1]), T.sem[args[2]], T.sem["sent"], pid, rid, sum(1 << x for x in eng))
                total["sent"] = total.get("sent", 0) + len(eng)
                s, inc = args[2], len(eng)
            else:
                s, inc = (o["extra"], 16) if o["kind"] == "d" else (esem[e], 1)
                fn = queue[e].dma_start if o["kind"] == "d" else call[name]
                fn(*[ap(x) for x in args], **{y: ap(x) for y, x in kw.items()}).then_inc(T.sem[s], inc)
            total[s] = total.get(s, 0) + inc
            done[i] = (s, total[s])
    for s in sorted(total):
        g.wait_ge(T.sem[s], total[s])
